import numpy as np
import ml_dtypes


def mxq(x, axis, fmt="e4m3"):
    dtype, down = {"e4m3": (ml_dtypes.float8_e4m3fn, 7), "e5m2": (ml_dtypes.float8_e5m2, 14)}[fmt]
    v = np.moveaxis(np.asarray(x, np.float32).astype(ml_dtypes.bfloat16).astype(np.float64), axis, -1)
    blocks = v.reshape(v.shape[:-1] + (-1, 32))
    amax = np.abs(blocks).max(-1, keepdims=True)
    byte = np.maximum(np.where(amax > 0, np.frexp(amax)[1] - 1 + 127, 0) - down, 1)
    scale = np.exp2(byte - 127.0)
    codes = (blocks / scale).astype(np.float32).astype(dtype).astype(np.float64)
    return np.moveaxis((codes * scale).reshape(v.shape), -1, axis)


WIDE = False


def mx_kscale(k):
    if not WIDE:
        return np.ones(k)
    levels = np.array([10, -10, 5, -5, 0])
    if k % 512:
        return np.exp2(np.random.permutation(np.resize(levels, k // 32))).repeat(32)
    a = np.empty((k // 512, 16))
    for p in range(k // 512):
        a[p, :8] = np.random.permutation(np.resize(levels, 8))
        for g in range(8):
            far = levels[np.abs(levels - a[p, g]) >= 10]
            a[p, g + 8] = far[np.random.randint(len(far))]
    return np.exp2(a.ravel()).repeat(32)


def f64(x):
    return np.asarray(x).astype(np.float64)


def striped(idx):
    return np.tile(idx.reshape(-1, 16).T, (8, 1)).astype(np.uint16)


def unstriped(offs):
    return offs[:16].T.reshape(-1).astype(np.int64)


def pack_weight(w):
    k, n = w.shape
    w = f64(np.asarray(w, np.float32).astype(ml_dtypes.bfloat16)).reshape(k // 32, 32, n)
    amax = np.abs(w).max(1)
    byte = np.clip(np.where(amax > 0, np.frexp(amax)[1] - 1 + 127 - 7, 1), 1, 254)
    scaled = (w * np.exp2(127.0 - byte)[:, None, :]).reshape(k, n).astype(np.float32)
    words = np.ascontiguousarray(scaled.reshape(k // 512, 128, 4, n).transpose(0, 1, 3, 2)).astype(ml_dtypes.float8_e4m3fn).view(np.uint8)
    return words, np.ascontiguousarray(byte.astype(np.uint8).reshape(k // 512, 16, n))


def unpack_weight(words, scales):
    g, p, n, _ = words.shape
    vals = np.ascontiguousarray(words).view(ml_dtypes.float8_e4m3fn).astype(np.float64) * np.repeat(np.exp2(scales.astype(np.float64) - 127.0), 8, axis=1)[..., None]
    return vals.transpose(0, 1, 3, 2).reshape(g * 512, n)


def planes(y):
    n, m = y.shape
    v = y.astype(np.float32).astype(ml_dtypes.bfloat16).astype(np.float64).reshape(n // 32, 32, m)
    top = np.abs(v).max(1)
    byte = np.clip(np.where(top > 0, np.frexp(top)[1] - 1 + 127 - 7, 1), 1, 254)
    codes = (v * np.exp2(127.0 - byte)[:, None, :]).reshape(n, m).astype(np.float32).astype(ml_dtypes.float8_e4m3fn).view(np.uint8)
    words = codes.reshape(n // 512, 128, 4, m).transpose(0, 1, 3, 2)
    return np.ascontiguousarray(words), np.ascontiguousarray(byte.astype(np.uint8).reshape(n // 512, 16, m))


def relu(v):
    return np.maximum(v, 0.0)


K, T, S, H, N = 512, 2048, 1024, 512, 512


def setup_inputs():
    n = np.random.standard_normal
    s = mx_kscale(K)[:, None]
    u = mx_kscale(H)
    packed_xT = pack_weight(n((K, T)) * s)
    return {
        "x_words": packed_xT[0],
        "x_scales": packed_xT[1],
        "w1": (n((K, H)) / np.sqrt(K) / s * u).astype(np.float32),
        "w2": (n((H, N)) / np.sqrt(2 * H) / u[:, None]).astype(np.float32),
        "w3": (n((K, N)) / np.sqrt(2 * K) / s).astype(np.float32),
        "offs": striped(np.random.permutation(T)[:S]),
    }


def reference(x_words, x_scales, w1, w2, w3, offs):
    xq = unpack_weight(x_words, x_scales)[:, unstriped(offs)]
    h = relu(mxq(f64(w1), 0, "e4m3").T @ xq)
    out_0 = mxq(f64(w2), 0, "e4m3").T @ mxq(h, 0, "e4m3") + mxq(f64(w3), 0, "e4m3").T @ xq
    return (out_0,) + planes(out_0)

@@ -1,0 +1,220 @@
+from contextlib import ExitStack
+
+import concourse.mybir as mybir
+
+K, T, S, H, N = 512, 2048, 1024, 512, 512
+FLOPS = 2 * S * (K * H + H * N + K * N)
+
+F32 = mybir.dt.float32
+BF16 = mybir.dt.bfloat16
+I32 = mybir.dt.int32
+U32 = mybir.dt.uint32
+U16 = mybir.dt.uint16
+U8 = mybir.dt.uint8
+FP8X4 = mybir.dt.float8_e4m3fn_x4
+RELU = mybir.ActivationFunctionType.Relu
+
+P = 128
+PACK = 4
+HALF = 512
+GATHER = 256
+H_TOKENS = 128
+
+
+def tile_picked_zskip_relu_po_kernel(
+    tc, x_words, x_scales, w1, w2, w3, offs, out_0, out_1, out_2
+):
+    nc = tc.nc
+    with ExitStack() as ctx:
+        keep = ctx.enter_context(tc.tile_pool(name="keep", bufs=1))
+        psum = ctx.enter_context(tc.psum_pool(name="psum", bufs=8))
+
+        def sbuf(name, shape, dtype):
+            return keep.tile(shape, dtype, name=name, align_bytes=64)
+
+        offsets = keep.tile([P, S // 16], U16, name="offsets")
+        nc.sync.dma_start(offsets[:], offs)
+
+        scale_window = sbuf("scale_window", [P, T], U8)
+        nc.vector.memset(scale_window[:].bitcast(I32), 0)
+        for q in range(4):
+            nc.sync.dma_start(
+                scale_window[32 * q : 32 * q + 4, :].bitcast(I32),
+                x_scales[0, 4 * q : 4 * q + 4, :].bitcast(I32),
+            )
+
+        raw = {}
+
+        def load_weight(name, w, pieces=1):
+            raw[name] = sbuf(name + "_raw", [P, PACK, 512], F32)
+            rows = w.rearrange("(p j) c -> p j c", j=PACK)
+            step = PACK // pieces
+            for j in range(0, PACK, step):
+                nc.sync.dma_start(raw[name][:, j : j + step, :], rows[:, j : j + step, :])
+
+        word_window = sbuf("word_window", [P, T], I32)
+        load_weight("w1", w1, 4)
+        nc.sync.dma_start(word_window[:], x_words[0].rearrange("p n t -> p (n t)").bitcast(I32))
+        load_weight("w3", w3)
+        load_weight("w2", w2)
+
+        x_codes = [sbuf("x_codes%d" % u, [P, HALF], U32) for u in range(2)]
+        x_bytes = [sbuf("x_bytes%d" % u, [P, HALF], U8) for u in range(2)]
+
+        def entries(start, count):
+            return offsets[:, start // 16 : (start + count) // 16]
+
+        def gather_scales(u):
+            nc.vector.tensor_copy(x_bytes[u][:], scale_window[:].indirect(entries(u * HALF, HALF)))
+
+        def gather_words(g):
+            u, c = divmod(g * GATHER, HALF)
+            nc.vector.tensor_copy(
+                x_codes[u][:, c : c + GATHER],
+                word_window[:].bitcast(U32).indirect(entries(g * GATHER, GATHER)),
+            )
+
+        rounded = {name: sbuf(name + "_bf16", [P, 512 * PACK], BF16) for name in ("w1", "w2", "w3")}
+        codes = {name: sbuf(name + "_codes", [P, 512], U32) for name in ("w1", "w2", "w3")}
+        scales = {name: sbuf(name + "_scales", [P, 512], U8) for name in ("w1", "w2", "w3")}
+
+        def round_weight(name, scalar_share):
+            src = raw[name][:].rearrange("p j (m t) -> p m j t", t=PACK)
+            dst = rounded[name][:].rearrange("p (t m j) -> p m j t", t=PACK, j=PACK)
+            cut = P - scalar_share
+            if scalar_share:
+                nc.scalar.copy(dst[:, cut:], src[:, cut:])
+            nc.vector.tensor_copy(dst[:, :cut], src[:, :cut])
+
+        def quantize(out_codes, out_scales, values, start, count):
+            nc.vector.quantize_mx(
+                out=out_codes[:, start : start + count].bitcast(FP8X4),
+                scales=out_scales[:, start : start + count],
+                in_=values[:, PACK * start : PACK * (start + count)],
+            )
+
+        def quantize_weight(name, pieces):
+            for i in range(pieces):
+                quantize(codes[name], scales[name], rounded[name], i * 512 // pieces, 512 // pieces)
+
+        def multiply(out, name, t, moving_codes, moving_scales, start, stop):
+            cols = slice(t * P, (t + 1) * P)
+            nc.tensor.matmul_mx(
+                out=out,
+                lhsT=codes[name][:, cols].bitcast(FP8X4),
+                lhsT_scale=scales[name][:, cols],
+                rhs=moving_codes.bitcast(FP8X4),
+                rhs_scale=moving_scales,
+                start=start,
+                stop=stop,
+            )
+
+        h_bf16 = [sbuf("h_bf16%d" % u, [P, HALF * PACK], BF16) for u in range(2)]
+        h_codes = [sbuf("h_codes%d" % u, [P, HALF], U32) for u in range(2)]
+        h_scales = [sbuf("h_scales%d" % u, [P, HALF], U8) for u in range(2)]
+        h_banks = {}
+
+        def hidden_product(b):
+            u, c = divmod(b * H_TOKENS, HALF)
+            cols = slice(c, c + H_TOKENS)
+            h_banks[b] = psum.tile([P, PACK, H_TOKENS], F32, name="h_bank", tag="bank")
+            for t in range(PACK):
+                multiply(h_banks[b][:, t, :], "w1", t, x_codes[u][:, cols], x_bytes[u][:, cols], True, True)
+
+        def hidden_out(b):
+            u, c = divmod(b * H_TOKENS, HALF)
+            nc.scalar.activation(
+                h_bf16[u][:, PACK * c : PACK * (c + H_TOKENS)].rearrange("p (n t) -> p n t", t=PACK),
+                h_banks[b][:].rearrange("p t n -> p n t"),
+                RELU,
+            )
+
+        y_banks = {}
+        y_f32 = [sbuf("y_f32%d" % u, [P, PACK, HALF], F32) for u in range(2)]
+        y_bf16 = [sbuf("y_bf16%d" % u, [P, HALF * PACK], BF16) for u in range(2)]
+        y_codes = [sbuf("y_codes%d" % u, [P, HALF], I32) for u in range(2)]
+        y_scales = sbuf("y_scales", [P, S], U8)
+        out_rows = out_0.rearrange("(p t) s -> p t s", t=PACK)
+        out_words = out_1[0].rearrange("p n t -> p (n t)").bitcast(I32)
+
+        def shortcut_product(u, t):
+            y_banks[u, t] = psum.tile([P, HALF], F32, name="y_bank", tag="bank")
+            multiply(y_banks[u, t][:], "w3", t, x_codes[u][:], x_bytes[u][:], True, False)
+
+        def branch_product(u, t):
+            multiply(y_banks[u, t][:], "w2", t, h_codes[u][:], h_scales[u][:], False, True)
+
+        def result_out(u, t, on_vector):
+            if on_vector:
+                nc.vector.tensor_copy(y_f32[u][:, t, :], y_banks[u, t][:])
+            else:
+                nc.scalar.copy(y_f32[u][:, t, :], y_banks[u, t][:])
+            nc.sync.dma_start(out_rows[:, t, u * HALF : (u + 1) * HALF], y_f32[u][:, t, :])
+
+        def round_result(u, c, count, copy=nc.vector.tensor_copy):
+            copy(
+                y_bf16[u][:, PACK * c : PACK * (c + count)].rearrange("p (g i t) -> p g t i", i=4, t=PACK),
+                y_f32[u][:, :, c : c + count].rearrange("p t (g i) -> p g t i", i=4),
+            )
+
+        def quantize_result(u, c, count):
+            nc.vector.quantize_mx(
+                out=y_codes[u][:, c : c + count].bitcast(FP8X4),
+                scales=y_scales[:, u * HALF + c : u * HALF + c + count],
+                in_=y_bf16[u][:, PACK * c : PACK * (c + count)],
+            )
+
+        def store_words(u, c, count):
+            nc.sync.dma_start(out_words[:, u * HALF + c : u * HALF + c + count], y_codes[u][:, c : c + count])
+
+        warm = sbuf("warm", [P, 1], F32)
+        nc.gpsimd.memset(warm[:], 0.0)
+        warm_out = sbuf("warm_out", [P, 1], F32)
+        nc.scalar.activation(warm_out[:], warm[:], RELU)
+        gather_scales(0)
+        gather_scales(1)
+        round_weight("w1", 96)
+        quantize_weight("w1", 1)
+        for g in range(4):
+            gather_words(g)
+            hidden_product(2 * g)
+            hidden_product(2 * g + 1)
+        for b in range(4):
+            hidden_out(b)
+        round_weight("w3", 0)
+        quantize_weight("w3", 1)
+        quantize(h_codes[0], h_scales[0], h_bf16[0], 0, HALF)
+        for t in range(PACK):
+            shortcut_product(0, t)
+        round_weight("w2", 40)
+        quantize_weight("w2", 2)
+        for b in range(4, 8):
+            hidden_out(b)
+        for t in range(PACK):
+            branch_product(0, t)
+        quantize(h_codes[1], h_scales[1], h_bf16[1], 0, HALF)
+        for t in range(PACK):
+            result_out(0, t, t == 1)
+        for t in range(PACK):
+            shortcut_product(1, t)
+        for t in range(PACK):
+            branch_product(1, t)
+        round_result(0, 0, HALF)
+        for t in range(PACK):
+            result_out(1, t, False)
+        quantize_result(0, 0, HALF)
+        store_words(0, 0, HALF)
+        round_result(1, 0, 256)
+        round_result(1, 384, 128, nc.scalar.copy)
+        round_result(1, 256, 128)
+        quantize_result(1, 0, 256)
+        store_words(1, 0, 256)
+        quantize_result(1, 256, 256)
+        store_words(1, 256, 256)
+
+        for q in range(4):
+            queue = nc.sync if q % 2 == 0 else nc.scalar
+            queue.dma_start(
+                out_2[0, 4 * q : 4 * q + 4, :].bitcast(I32),
+                y_scales[32 * q : 32 * q + 4, :].bitcast(I32),
+            )

@@ -27,10 +27,10 @@ def tile_picked_zskip_relu_po_kernel(
     nc = tc.nc
     with ExitStack() as ctx:
         keep = ctx.enter_context(tc.tile_pool(name="keep", bufs=1))
-        psum = ctx.enter_context(tc.psum_pool(name="psum", bufs=8))
+        psum = ctx.enter_context(tc.psum_pool(name="psum", bufs=4))
 
-        def sbuf(name, shape, dtype):
-            return keep.tile(shape, dtype, name=name, align_bytes=64)
+        def sbuf(name, shape, dtype, tag=""):
+            return keep.tile(shape, dtype, name=name, tag=tag or name, align_bytes=64)
 
         offsets = keep.tile([P, S // 16], U16, name="offsets")
         nc.sync.dma_start(offsets[:], offs)
@@ -45,46 +45,44 @@ def tile_picked_zskip_relu_po_kernel(
 
         raw = {}
 
-        def load_weight(name, w, pieces=1):
+        def load_weight(name, w, pieces=((0, PACK),)):
             raw[name] = sbuf(name + "_raw", [P, PACK, 512], F32)
             rows = w.rearrange("(p j) c -> p j c", j=PACK)
-            step = PACK // pieces
-            for j in range(0, PACK, step):
-                nc.sync.dma_start(raw[name][:, j : j + step, :], rows[:, j : j + step, :])
+            for first, last in pieces:
+                nc.sync.dma_start(raw[name][:, first:last, :], rows[:, first:last, :])
 
         word_window = sbuf("word_window", [P, T], I32)
-        load_weight("w1", w1, 4)
+        load_weight("w1", w1, ((0, 1), (1, PACK)))
         nc.sync.dma_start(word_window[:], x_words[0].rearrange("p n t -> p (n t)").bitcast(I32))
         load_weight("w3", w3)
         load_weight("w2", w2)
 
         x_codes = [sbuf("x_codes%d" % u, [P, HALF], U32) for u in range(2)]
-        x_bytes = [sbuf("x_bytes%d" % u, [P, HALF], U8) for u in range(2)]
+        x_all_bytes = sbuf("x_bytes", [P, S], U8)
+        x_bytes = [x_all_bytes[:, u * HALF : (u + 1) * HALF] for u in range(2)]
 
         def entries(start, count):
             return offsets[:, start // 16 : (start + count) // 16]
 
-        def gather_scales(u):
-            nc.vector.tensor_copy(x_bytes[u][:], scale_window[:].indirect(entries(u * HALF, HALF)))
+        def gather_scales():
+            nc.vector.tensor_copy(x_all_bytes[:], scale_window[:].indirect(offsets[:]))
 
-        def gather_words(g):
-            u, c = divmod(g * GATHER, HALF)
+        def gather_words(start, count):
+            u, c = divmod(start, HALF)
             nc.vector.tensor_copy(
-                x_codes[u][:, c : c + GATHER],
-                word_window[:].bitcast(U32).indirect(entries(g * GATHER, GATHER)),
+                x_codes[u][:, c : c + count],
+                word_window[:].bitcast(U32).indirect(entries(start, count)),
             )
 
-        rounded = {name: sbuf(name + "_bf16", [P, 512 * PACK], BF16) for name in ("w1", "w2", "w3")}
+        rounded = {}
         codes = {name: sbuf(name + "_codes", [P, 512], U32) for name in ("w1", "w2", "w3")}
         scales = {name: sbuf(name + "_scales", [P, 512], U8) for name in ("w1", "w2", "w3")}
 
-        def round_weight(name, scalar_share):
+        def round_weight(name, pair, copy, tag=""):
+            rounded[name, pair] = sbuf("%s_bf16_%d" % (name, pair), [P, 256 * PACK], BF16, tag)
             src = raw[name][:].rearrange("p j (m t) -> p m j t", t=PACK)
-            dst = rounded[name][:].rearrange("p (t m j) -> p m j t", t=PACK, j=PACK)
-            cut = P - scalar_share
-            if scalar_share:
-                nc.scalar.copy(dst[:, cut:], src[:, cut:])
-            nc.vector.tensor_copy(dst[:, :cut], src[:, :cut])
+            dst = rounded[name, pair][:].rearrange("p (t m j) -> p m j t", t=2, j=PACK)
+            copy(dst, src[:, :, :, 2 * pair : 2 * pair + 2])
 
         def quantize(out_codes, out_scales, values, start, count):
             nc.vector.quantize_mx(
@@ -93,9 +91,11 @@ def tile_picked_zskip_relu_po_kernel(
                 in_=values[:, PACK * start : PACK * (start + count)],
             )
 
-        def quantize_weight(name, pieces):
-            for i in range(pieces):
-                quantize(codes[name], scales[name], rounded[name], i * 512 // pieces, 512 // pieces)
+        def quantize_weight(name, pair):
+            cols = slice(256 * pair, 256 * (pair + 1))
+            nc.vector.quantize_mx(
+                out=codes[name][:, cols].bitcast(FP8X4), scales=scales[name][:, cols], in_=rounded[name, pair][:]
+            )
 
         def multiply(out, name, t, moving_codes, moving_scales, start, stop):
             cols = slice(t * P, (t + 1) * P)
@@ -110,14 +110,14 @@ def tile_picked_zskip_relu_po_kernel(
             )
 
         h_bf16 = [sbuf("h_bf16%d" % u, [P, HALF * PACK], BF16) for u in range(2)]
-        h_codes = [sbuf("h_codes%d" % u, [P, HALF], U32) for u in range(2)]
+        h_codes = [sbuf("h_codes0", [P, HALF], U32)]
         h_scales = [sbuf("h_scales%d" % u, [P, HALF], U8) for u in range(2)]
         h_banks = {}
 
         def hidden_product(b):
             u, c = divmod(b * H_TOKENS, HALF)
             cols = slice(c, c + H_TOKENS)
-            h_banks[b] = psum.tile([P, PACK, H_TOKENS], F32, name="h_bank", tag="bank")
+            h_banks[b] = psum.tile([P, PACK, H_TOKENS], F32, name="h_bank", tag="early")
             for t in range(PACK):
                 multiply(h_banks[b][:, t, :], "w1", t, x_codes[u][:, cols], x_bytes[u][:, cols], True, True)
 
@@ -138,7 +138,7 @@ def tile_picked_zskip_relu_po_kernel(
         out_words = out_1[0].rearrange("p n t -> p (n t)").bitcast(I32)
 
         def shortcut_product(u, t):
-            y_banks[u, t] = psum.tile([P, HALF], F32, name="y_bank", tag="bank")
+            y_banks[u, t] = psum.tile([P, HALF], F32, name="y_bank", tag="early" if (u == 1 and t < 2) else "late")
             multiply(y_banks[u, t][:], "w3", t, x_codes[u][:], x_bytes[u][:], True, False)
 
         def branch_product(u, t):
@@ -171,30 +171,38 @@ def tile_picked_zskip_relu_po_kernel(
         nc.gpsimd.memset(warm[:], 0.0)
         warm_out = sbuf("warm_out", [P, 1], F32)
         nc.scalar.activation(warm_out[:], warm[:], RELU)
-        gather_scales(0)
-        gather_scales(1)
-        round_weight("w1", 96)
+        gather_scales()
+        round_weight("w1", 1, nc.scalar.copy)
+        round_weight("w1", 0, nc.vector.tensor_copy)
         quantize_weight("w1", 1)
-        for g in range(4):
-            gather_words(g)
-            hidden_product(2 * g)
-            hidden_product(2 * g + 1)
+        quantize_weight("w1", 0)
+        gather_words(0, 256)
+        gather_words(256, 256)
+        gather_words(512, 512)
+        for b in range(4):
+            hidden_product(b)
         for b in range(4):
             hidden_out(b)
-        round_weight("w3", 0)
+        for b in range(4, 8):
+            hidden_product(b)
+            hidden_out(b)
+        round_weight("w3", 0, nc.vector.tensor_copy)
+        round_weight("w3", 1, nc.vector.tensor_copy)
+        quantize_weight("w3", 0)
         quantize_weight("w3", 1)
-        quantize(h_codes[0], h_scales[0], h_bf16[0], 0, HALF)
         for t in range(PACK):
             shortcut_product(0, t)
-        round_weight("w2", 40)
-        quantize_weight("w2", 2)
-        for b in range(4, 8):
-            hidden_out(b)
-        for t in range(PACK):
-            branch_product(0, t)
+        round_weight("w2", 0, nc.vector.tensor_copy, "w2_stage")
+        quantize(h_codes[0], h_scales[0], h_bf16[0], 0, HALF)
+        quantize_weight("w2", 0)
+        round_weight("w2", 1, nc.vector.tensor_copy, "w2_stage")
+        quantize_weight("w2", 1)
+        h_codes.append(sbuf("h_codes1", [P, HALF], U32, tag="w2_raw"))
         quantize(h_codes[1], h_scales[1], h_bf16[1], 0, HALF)
         for t in range(PACK):
-            result_out(0, t, t == 1)
+            branch_product(0, t)
+        for t in range(PACK):
+            result_out(0, t, t == 3)
         for t in range(PACK):
             shortcut_product(1, t)
         for t in range(PACK):
@@ -205,8 +213,8 @@ def tile_picked_zskip_relu_po_kernel(
         quantize_result(0, 0, HALF)
         store_words(0, 0, HALF)
         round_result(1, 0, 256)
-        round_result(1, 384, 128, nc.scalar.copy)
-        round_result(1, 256, 128)
+        round_result(1, 320, 192, nc.scalar.copy)
+        round_result(1, 256, 64)
         quantize_result(1, 0, 256)
         store_words(1, 0, 256)
         quantize_result(1, 256, 256)

@@ -27,10 +27,13 @@ def tile_picked_zskip_relu_po_kernel(
     nc = tc.nc
     with ExitStack() as ctx:
         keep = ctx.enter_context(tc.tile_pool(name="keep", bufs=1))
-        psum = ctx.enter_context(tc.psum_pool(name="psum", bufs=4))
+        psum = ctx.enter_context(tc.psum_pool(name="psum", bufs=1))
 
         def sbuf(name, shape, dtype, tag=""):
             return keep.tile(shape, dtype, name=name, tag=tag or name, align_bytes=64)
+
+        def bank(number, sums, tokens):
+            return psum.tile([P, sums, tokens], F32, name="bank", tag="bank%d" % number)
 
         offsets = keep.tile([P, S // 16], U16, name="offsets")
         nc.sync.dma_start(offsets[:], offs)
@@ -57,45 +60,54 @@ def tile_picked_zskip_relu_po_kernel(
         load_weight("w3", w3)
         load_weight("w2", w2)
 
+        warm = sbuf("warm", [P, 1], F32)
+        nc.gpsimd.memset(warm[:], 0.0)
+        warm_out = sbuf("warm_out", [P, 1], F32)
+        nc.scalar.activation(warm_out[:], warm[:], RELU)
+
         x_codes = [sbuf("x_codes%d" % u, [P, HALF], U32) for u in range(2)]
-        x_all_bytes = sbuf("x_bytes", [P, S], U8)
-        x_bytes = [x_all_bytes[:, u * HALF : (u + 1) * HALF] for u in range(2)]
+        x_bytes = sbuf("x_bytes", [P, S], U8)
 
-        def entries(start, count):
-            return offsets[:, start // 16 : (start + count) // 16]
-
-        def gather_scales():
-            nc.vector.tensor_copy(x_all_bytes[:], scale_window[:].indirect(offsets[:]))
+        def gather_scales(start, count):
+            nc.vector.tensor_copy(
+                x_bytes[:, start : start + count],
+                scale_window[:].indirect(offsets[:, start // 16 : (start + count) // 16]),
+            )
 
         def gather_words(start, count):
             u, c = divmod(start, HALF)
             nc.vector.tensor_copy(
                 x_codes[u][:, c : c + count],
-                word_window[:].bitcast(U32).indirect(entries(start, count)),
+                word_window[:].bitcast(U32).indirect(offsets[:, start // 16 : (start + count) // 16]),
             )
 
         rounded = {}
         codes = {name: sbuf(name + "_codes", [P, 512], U32) for name in ("w1", "w2", "w3")}
         scales = {name: sbuf(name + "_scales", [P, 512], U8) for name in ("w1", "w2", "w3")}
 
-        def round_weight(name, pair, copy, tag=""):
-            rounded[name, pair] = sbuf("%s_bf16_%d" % (name, pair), [P, 256 * PACK], BF16, tag)
+        def round_whole(name):
+            rounded[name] = sbuf(name + "_bf16", [P, 512 * PACK], BF16)
+            nc.vector.tensor_copy(
+                rounded[name][:].rearrange("p (t m j) -> p m j t", t=PACK, j=PACK),
+                raw[name][:].rearrange("p j (m t) -> p m j t", t=PACK),
+            )
+
+        def round_weight(name, pair, copy, tag="", first=0, last=P):
+            if (name, pair) not in rounded:
+                rounded[name, pair] = sbuf("%s_bf16_%d" % (name, pair), [P, 256 * PACK], BF16, tag)
             src = raw[name][:].rearrange("p j (m t) -> p m j t", t=PACK)
             dst = rounded[name, pair][:].rearrange("p (t m j) -> p m j t", t=2, j=PACK)
-            copy(dst, src[:, :, :, 2 * pair : 2 * pair + 2])
+            copy(dst[:, first:last], src[:, first:last, :, 2 * pair : 2 * pair + 2])
 
-        def quantize(out_codes, out_scales, values, start, count):
-            nc.vector.quantize_mx(
-                out=out_codes[:, start : start + count].bitcast(FP8X4),
-                scales=out_scales[:, start : start + count],
-                in_=values[:, PACK * start : PACK * (start + count)],
-            )
+        def quantize(out_codes, out_scales, values):
+            nc.vector.quantize_mx(out=out_codes.bitcast(FP8X4), scales=out_scales, in_=values)
 
         def quantize_weight(name, pair):
             cols = slice(256 * pair, 256 * (pair + 1))
-            nc.vector.quantize_mx(
-                out=codes[name][:, cols].bitcast(FP8X4), scales=scales[name][:, cols], in_=rounded[name, pair][:]
-            )
+            quantize(codes[name][:, cols], scales[name][:, cols], rounded[name, pair][:])
+
+        def quantize_whole(name):
+            quantize(codes[name][:], scales[name][:], rounded[name][:])
 
         def multiply(out, name, t, moving_codes, moving_scales, start, stop):
             cols = slice(t * P, (t + 1) * P)
@@ -109,25 +121,38 @@ def tile_picked_zskip_relu_po_kernel(
                 stop=stop,
             )
 
+        def x_operand(start, count):
+            u, c = divmod(start, HALF)
+            return x_codes[u][:, c : c + count], x_bytes[:, start : start + count]
+
         h_bf16 = [sbuf("h_bf16%d" % u, [P, HALF * PACK], BF16) for u in range(2)]
-        h_codes = [sbuf("h_codes0", [P, HALF], U32)]
-        h_scales = [sbuf("h_scales%d" % u, [P, HALF], U8) for u in range(2)]
+        h_codes = {}
+        h_scales = sbuf("h_scales", [P, S], U8)
         h_banks = {}
 
-        def hidden_product(b):
-            u, c = divmod(b * H_TOKENS, HALF)
-            cols = slice(c, c + H_TOKENS)
-            h_banks[b] = psum.tile([P, PACK, H_TOKENS], F32, name="h_bank", tag="early")
+        def hidden_product(b, number):
+            h_banks[b] = bank(number, PACK, H_TOKENS)
             for t in range(PACK):
-                multiply(h_banks[b][:, t, :], "w1", t, x_codes[u][:, cols], x_bytes[u][:, cols], True, True)
+                multiply(h_banks[b][:, t, :], "w1", t, *x_operand(b * H_TOKENS, H_TOKENS), True, True)
 
-        def hidden_out(b):
+        def hidden_out(b, on_vector=False):
             u, c = divmod(b * H_TOKENS, HALF)
-            nc.scalar.activation(
-                h_bf16[u][:, PACK * c : PACK * (c + H_TOKENS)].rearrange("p (n t) -> p n t", t=PACK),
-                h_banks[b][:].rearrange("p t n -> p n t"),
-                RELU,
-            )
+            dst = h_bf16[u][:, PACK * c : PACK * (c + H_TOKENS)].rearrange("p (n t) -> p n t", t=PACK)
+            src = h_banks[b][:].rearrange("p t n -> p n t")
+            if on_vector:
+                nc.vector.tensor_scalar_max(dst, src, 0.0)
+            else:
+                nc.scalar.activation(dst, src, RELU)
+
+        def quantize_hidden(start, count, tag=""):
+            u, c = divmod(start, HALF)
+            if u not in h_codes:
+                h_codes[u] = sbuf("h_codes%d" % u, [P, HALF], U32, tag)
+            quantize(h_codes[u][:, c : c + count], h_scales[:, start : start + count], h_bf16[u][:, PACK * c : PACK * (c + count)])
+
+        def h_operand(start, count):
+            u, c = divmod(start, HALF)
+            return h_codes[u][:, c : c + count], h_scales[:, start : start + count]
 
         y_banks = {}
         y_f32 = [sbuf("y_f32%d" % u, [P, PACK, HALF], F32) for u in range(2)]
@@ -137,88 +162,101 @@ def tile_picked_zskip_relu_po_kernel(
         out_rows = out_0.rearrange("(p t) s -> p t s", t=PACK)
         out_words = out_1[0].rearrange("p n t -> p (n t)").bitcast(I32)
 
-        def shortcut_product(u, t):
-            y_banks[u, t] = psum.tile([P, HALF], F32, name="y_bank", tag="early" if (u == 1 and t < 2) else "late")
-            multiply(y_banks[u, t][:], "w3", t, x_codes[u][:], x_bytes[u][:], True, False)
+        def shortcut_product(first, sums, start, number):
+            count = HALF // sums
+            y_banks[first, start] = bank(number, sums, count)
+            for i in range(sums):
+                multiply(y_banks[first, start][:, i, :], "w3", first + i, *x_operand(start, count), i == 0, False)
 
-        def branch_product(u, t):
-            multiply(y_banks[u, t][:], "w2", t, h_codes[u][:], h_scales[u][:], False, True)
+        def branch_product(first, sums, start):
+            count = HALF // sums
+            for i in range(sums):
+                multiply(y_banks[first, start][:, i, :], "w2", first + i, *h_operand(start, count), False, i == sums - 1)
 
-        def result_out(u, t, on_vector):
-            if on_vector:
-                nc.vector.tensor_copy(y_f32[u][:, t, :], y_banks[u, t][:])
-            else:
-                nc.scalar.copy(y_f32[u][:, t, :], y_banks[u, t][:])
-            nc.sync.dma_start(out_rows[:, t, u * HALF : (u + 1) * HALF], y_f32[u][:, t, :])
+        def result_out(first, sums, start, copy):
+            u, c = divmod(start, HALF)
+            copy(y_f32[u][:, first : first + sums, c : c + HALF // sums], y_banks[first, start][:])
 
-        def round_result(u, c, count, copy=nc.vector.tensor_copy):
+        def store_result(first, sums, start, count, queue=nc.sync):
+            u, c = divmod(start, HALF)
+            queue.dma_start(
+                out_rows[:, first : first + sums, start : start + count], y_f32[u][:, first : first + sums, c : c + count]
+            )
+
+        def round_result(start, count, copy=nc.vector.tensor_copy):
+            u, c = divmod(start, HALF)
             copy(
                 y_bf16[u][:, PACK * c : PACK * (c + count)].rearrange("p (g i t) -> p g t i", i=4, t=PACK),
                 y_f32[u][:, :, c : c + count].rearrange("p t (g i) -> p g t i", i=4),
             )
 
-        def quantize_result(u, c, count):
-            nc.vector.quantize_mx(
-                out=y_codes[u][:, c : c + count].bitcast(FP8X4),
-                scales=y_scales[:, u * HALF + c : u * HALF + c + count],
-                in_=y_bf16[u][:, PACK * c : PACK * (c + count)],
+        def quantize_result(start, count):
+            u, c = divmod(start, HALF)
+            quantize(
+                y_codes[u][:, c : c + count],
+                y_scales[:, start : start + count],
+                y_bf16[u][:, PACK * c : PACK * (c + count)],
             )
 
-        def store_words(u, c, count):
-            nc.sync.dma_start(out_words[:, u * HALF + c : u * HALF + c + count], y_codes[u][:, c : c + count])
+        def store_words(start, count, queue=nc.sync):
+            u, c = divmod(start, HALF)
+            queue.dma_start(out_words[:, start : start + count], y_codes[u][:, c : c + count])
 
-        warm = sbuf("warm", [P, 1], F32)
-        nc.gpsimd.memset(warm[:], 0.0)
-        warm_out = sbuf("warm_out", [P, 1], F32)
-        nc.scalar.activation(warm_out[:], warm[:], RELU)
-        gather_scales()
-        round_weight("w1", 1, nc.scalar.copy)
-        round_weight("w1", 0, nc.vector.tensor_copy)
+        vector_copy, scalar_copy = nc.vector.tensor_copy, nc.scalar.copy
+        gather_scales(0, S)
+        round_weight("w1", 1, scalar_copy)
+        round_weight("w1", 0, scalar_copy, "", 88, P)
+        round_weight("w1", 0, vector_copy, "", 0, 88)
         quantize_weight("w1", 1)
         quantize_weight("w1", 0)
         gather_words(0, 256)
         gather_words(256, 256)
         gather_words(512, 512)
-        for b in range(4):
-            hidden_product(b)
-        for b in range(4):
+        for b in range(6):
+            hidden_product(b, b % 4)
             hidden_out(b)
-        for b in range(4, 8):
-            hidden_product(b)
-            hidden_out(b)
-        round_weight("w3", 0, nc.vector.tensor_copy)
-        round_weight("w3", 1, nc.vector.tensor_copy)
-        quantize_weight("w3", 0)
-        quantize_weight("w3", 1)
+        round_whole("w3")
+        quantize_hidden(0, HALF)
+        quantize_whole("w3")
         for t in range(PACK):
-            shortcut_product(0, t)
-        round_weight("w2", 0, nc.vector.tensor_copy, "w2_stage")
-        quantize(h_codes[0], h_scales[0], h_bf16[0], 0, HALF)
+            shortcut_product(t, 1, 0, 4 + t)
+        round_weight("w2", 0, vector_copy)
+        round_weight("w2", 1, scalar_copy, "", 40, P)
+        round_weight("w2", 1, vector_copy, "", 0, 40)
         quantize_weight("w2", 0)
-        round_weight("w2", 1, nc.vector.tensor_copy, "w2_stage")
+        branch_product(0, 1, 0)
+        branch_product(1, 1, 0)
         quantize_weight("w2", 1)
-        h_codes.append(sbuf("h_codes1", [P, HALF], U32, tag="w2_raw"))
-        quantize(h_codes[1], h_scales[1], h_bf16[1], 0, HALF)
-        for t in range(PACK):
-            branch_product(0, t)
-        for t in range(PACK):
-            result_out(0, t, t == 3)
-        for t in range(PACK):
-            shortcut_product(1, t)
-        for t in range(PACK):
-            branch_product(1, t)
-        round_result(0, 0, HALF)
-        for t in range(PACK):
-            result_out(1, t, False)
-        quantize_result(0, 0, HALF)
-        store_words(0, 0, HALF)
-        round_result(1, 0, 256)
-        round_result(1, 320, 192, nc.scalar.copy)
-        round_result(1, 256, 64)
-        quantize_result(1, 0, 256)
-        store_words(1, 0, 256)
-        quantize_result(1, 256, 256)
-        store_words(1, 256, 256)
+        branch_product(2, 1, 0)
+        branch_product(3, 1, 0)
+        for b in range(6, 8):
+            hidden_product(b, b % 4)
+            hidden_out(b)
+        quantize_hidden(512, HALF, "w2_bf16_0")
+        for c in (0, 256):
+            scalar_copy(y_f32[0][:, 0, c : c + 256], y_banks[0, 0][:, 0, c : c + 256])
+            store_result(0, 1, c, 256)
+        result_out(1, 1, 0, scalar_copy)
+        store_result(1, 1, 0, HALF)
+        result_out(2, 1, 0, vector_copy)
+        store_result(2, 1, 0, HALF)
+        result_out(3, 1, 0, scalar_copy)
+        store_result(3, 1, 0, HALF)
+        for b in range(4):
+            shortcut_product(0, 4, HALF + b * H_TOKENS, b)
+            branch_product(0, 4, HALF + b * H_TOKENS)
+            result_out(0, 4, HALF + b * H_TOKENS, scalar_copy)
+            if b % 2 == 1:
+                store_result(0, 4, HALF + (b - 1) * H_TOKENS, 256)
+        round_result(0, HALF)
+        round_result(512, 256)
+        quantize_result(0, HALF)
+        store_words(0, HALF)
+        round_result(768, 128)
+        round_result(896, 128, scalar_copy)
+        quantize_result(512, 256)
+        quantize_result(768, 256)
+        store_words(512, HALF)
 
         for q in range(4):
             queue = nc.sync if q % 2 == 0 else nc.scalar

@@ -82,7 +82,7 @@ def tile_picked_zskip_relu_po_kernel(
             )
 
         rounded = {}
-        codes = {name: sbuf(name + "_codes", [P, 512], U32) for name in ("w1", "w2", "w3")}
+        codes = {name: sbuf(name + "_codes", [P, 512], U32) for name in ("w1", "w3")}
         scales = {name: sbuf(name + "_scales", [P, 512], U8) for name in ("w1", "w2", "w3")}
 
         def round_whole(name):
@@ -173,6 +173,14 @@ def tile_picked_zskip_relu_po_kernel(
             for i in range(sums):
                 multiply(y_banks[first, start][:, i, :], "w2", first + i, *h_operand(start, count), False, i == sums - 1)
 
+        def late_product(first, sums, start, number):
+            count = HALF // sums
+            y_banks[first, start] = bank(number, sums, count)
+            for i in range(sums):
+                out = y_banks[first, start][:, i, :]
+                multiply(out, "w2", first + i, *h_operand(start, count), True, False)
+                multiply(out, "w3", first + i, *x_operand(start, count), False, True)
+
         def result_out(first, sums, start, copy):
             u, c = divmod(start, HALF)
             copy(y_f32[u][:, first : first + sums, c : c + HALF // sums], y_banks[first, start][:])
@@ -205,55 +213,54 @@ def tile_picked_zskip_relu_po_kernel(
         vector_copy, scalar_copy = nc.vector.tensor_copy, nc.scalar.copy
         gather_scales(0, S)
         round_weight("w1", 1, scalar_copy)
-        round_weight("w1", 0, scalar_copy, "", 88, P)
-        round_weight("w1", 0, vector_copy, "", 0, 88)
+        round_weight("w1", 0, vector_copy)
         quantize_weight("w1", 1)
         quantize_weight("w1", 0)
         gather_words(0, 256)
         gather_words(256, 256)
         gather_words(512, 512)
-        for b in range(6):
+        for b in range(8):
             hidden_product(b, b % 4)
             hidden_out(b)
-        round_whole("w3")
-        quantize_hidden(0, HALF)
-        quantize_whole("w3")
+        round_weight("w3", 0, vector_copy)
+        round_weight("w3", 1, vector_copy)
+        quantize_weight("w3", 0)
+        quantize_weight("w3", 1)
         for t in range(PACK):
             shortcut_product(t, 1, 0, 4 + t)
         round_weight("w2", 0, vector_copy)
-        round_weight("w2", 1, scalar_copy, "", 40, P)
-        round_weight("w2", 1, vector_copy, "", 0, 40)
+        quantize_hidden(0, HALF)
+        codes["w2"] = sbuf("w2_codes", [P, 512], U32, "w1_codes")
         quantize_weight("w2", 0)
         branch_product(0, 1, 0)
         branch_product(1, 1, 0)
+        round_weight("w2", 1, vector_copy, "w1_scales")
         quantize_weight("w2", 1)
+        quantize_hidden(512, HALF)
         branch_product(2, 1, 0)
         branch_product(3, 1, 0)
-        for b in range(6, 8):
-            hidden_product(b, b % 4)
-            hidden_out(b)
-        quantize_hidden(512, HALF, "w2_bf16_0")
-        for c in (0, 256):
-            scalar_copy(y_f32[0][:, 0, c : c + 256], y_banks[0, 0][:, 0, c : c + 256])
-            store_result(0, 1, c, 256)
+        result_out(0, 1, 0, scalar_copy)
+        store_result(0, 1, 0, HALF)
         result_out(1, 1, 0, scalar_copy)
         store_result(1, 1, 0, HALF)
-        result_out(2, 1, 0, vector_copy)
+        result_out(2, 1, 0, scalar_copy)
         store_result(2, 1, 0, HALF)
-        result_out(3, 1, 0, scalar_copy)
+        result_out(3, 1, 0, vector_copy)
         store_result(3, 1, 0, HALF)
-        for b in range(4):
-            shortcut_product(0, 4, HALF + b * H_TOKENS, b)
-            branch_product(0, 4, HALF + b * H_TOKENS)
-            result_out(0, 4, HALF + b * H_TOKENS, scalar_copy)
-            if b % 2 == 1:
-                store_result(0, 4, HALF + (b - 1) * H_TOKENS, 256)
+        for t in range(2):
+            late_product(t, 1, HALF, t)
+            result_out(t, 1, HALF, scalar_copy)
+            store_result(t, 1, HALF, HALF)
+        for start, number in ((512, 2), (768, 3)):
+            late_product(2, 2, start, number)
+            result_out(2, 2, start, scalar_copy)
+        store_result(2, 2, HALF, HALF)
         round_result(0, HALF)
         round_result(512, 256)
         quantize_result(0, HALF)
         store_words(0, HALF)
-        round_result(768, 128)
-        round_result(896, 128, scalar_copy)
+        round_result(768, 96)
+        round_result(864, 160, scalar_copy)
         quantize_result(512, 256)
         quantize_result(768, 256)
         store_words(512, HALF)

@@ -239,8 +239,9 @@ def tile_picked_zskip_relu_po_kernel(
         quantize_hidden(512, HALF)
         branch_product(2, 1, 0)
         branch_product(3, 1, 0)
-        result_out(0, 1, 0, scalar_copy)
-        store_result(0, 1, 0, HALF)
+        for c in (0, 256):
+            scalar_copy(y_f32[0][:, 0, c : c + 256], y_banks[0, 0][:, 0, c : c + 256])
+            store_result(0, 1, c, 256)
         result_out(1, 1, 0, scalar_copy)
         store_result(1, 1, 0, HALF)
         result_out(2, 1, 0, scalar_copy)

@@ -242,14 +242,15 @@ def tile_picked_zskip_relu_po_kernel(
         for c in (0, 256):
             scalar_copy(y_f32[0][:, 0, c : c + 256], y_banks[0, 0][:, 0, c : c + 256])
             store_result(0, 1, c, 256)
-        result_out(1, 1, 0, scalar_copy)
+        result_out(1, 1, 0, vector_copy)
         store_result(1, 1, 0, HALF)
         result_out(2, 1, 0, scalar_copy)
         store_result(2, 1, 0, HALF)
         result_out(3, 1, 0, vector_copy)
         store_result(3, 1, 0, HALF)
         for t in range(2):
-            late_product(t, 1, HALF, t)
+            shortcut_product(t, 1, HALF, t)
+            branch_product(t, 1, HALF)
             result_out(t, 1, HALF, scalar_copy)
             store_result(t, 1, HALF, HALF)
         for start, number in ((512, 2), (768, 3)):
@@ -260,8 +261,8 @@ def tile_picked_zskip_relu_po_kernel(
         round_result(512, 256)
         quantize_result(0, HALF)
         store_words(0, HALF)
-        round_result(768, 96)
-        round_result(864, 160, scalar_copy)
+        round_result(768, 64)
+        round_result(832, 192, scalar_copy)
         quantize_result(512, 256)
         quantize_result(768, 256)
         store_words(512, HALF)

@@ -19,6 +19,7 @@ PACK = 4
 HALF = 512
 GATHER = 256
 H_TOKENS = 128
+EARLY = 512
 
 
 def tile_picked_zskip_relu_po_kernel(
@@ -39,26 +40,24 @@ def tile_picked_zskip_relu_po_kernel(
         nc.sync.dma_start(offsets[:], offs)
 
         scale_window = sbuf("scale_window", [P, T], U8)
-        nc.vector.memset(scale_window[:].bitcast(I32), 0)
-        for q in range(4):
-            nc.sync.dma_start(
-                scale_window[32 * q : 32 * q + 4, :].bitcast(I32),
-                x_scales[0, 4 * q : 4 * q + 4, :].bitcast(I32),
-            )
+        nc.sync.dma_start(scale_window[16:32, :].bitcast(I32), x_scales[0].bitcast(I32))
+        for first, last in ((0, 16), (32, 64), (64, P)):
+            nc.vector.memset(scale_window[first:last, :].bitcast(I32), 0)
+        x_bytes = sbuf("x_bytes", [P, S], U8)
+        nc.vector.memset(x_bytes[:].bitcast(I32), 0)
 
+        space = sbuf("raw", [P, 2 * PACK * 512], F32)
         raw = {}
 
-        def load_weight(name, w, pieces=((0, PACK),)):
-            raw[name] = sbuf(name + "_raw", [P, PACK, 512], F32)
-            rows = w.rearrange("(p j) c -> p j c", j=PACK)
-            for first, last in pieces:
-                nc.sync.dma_start(raw[name][:, first:last, :], rows[:, first:last, :])
+        def load_weight(name, w, offset, first=0, last=PACK * 512):
+            raw[name] = space[:, offset : offset + PACK * 512].rearrange("p (j c) -> p j c", j=PACK)
+            rows = w.rearrange("(p j) c -> p (j c)", j=PACK)
+            nc.sync.dma_start(space[:, offset + first : offset + last], rows[:, first:last])
 
         word_window = sbuf("word_window", [P, T], I32)
-        load_weight("w1", w1, ((0, 1), (1, PACK)))
+        load_weight("w1", w1, PACK * 512 - 32)
         nc.sync.dma_start(word_window[:], x_words[0].rearrange("p n t -> p (n t)").bitcast(I32))
-        load_weight("w3", w3)
-        load_weight("w2", w2)
+        load_weight("w3", w3, 0, 0, EARLY)
 
         warm = sbuf("warm", [P, 1], F32)
         nc.gpsimd.memset(warm[:], 0.0)
@@ -66,11 +65,18 @@ def tile_picked_zskip_relu_po_kernel(
         nc.scalar.activation(warm_out[:], warm[:], RELU)
 
         x_codes = [sbuf("x_codes%d" % u, [P, HALF], U32) for u in range(2)]
-        x_bytes = sbuf("x_bytes", [P, S], U8)
+        picked_bytes = sbuf("picked_bytes", [P, S], U8)
+
+        def place_scales(start, count):
+            for q in range(4):
+                nc.sync.dma_start(
+                    x_bytes[32 * q : 32 * q + 4, start : start + count].bitcast(I32),
+                    picked_bytes[16 + 4 * q : 20 + 4 * q, start : start + count].bitcast(I32),
+                )
 
         def gather_scales(start, count):
             nc.vector.tensor_copy(
-                x_bytes[:, start : start + count],
+                picked_bytes[:, start : start + count],
                 scale_window[:].indirect(offsets[:, start // 16 : (start + count) // 16]),
             )
 
@@ -82,39 +88,31 @@ def tile_picked_zskip_relu_po_kernel(
             )
 
         rounded = {}
-        codes = {name: sbuf(name + "_codes", [P, 512], U32) for name in ("w1", "w3")}
-        scales = {name: sbuf(name + "_scales", [P, 512], U8) for name in ("w1", "w2", "w3")}
-
-        def round_whole(name):
-            rounded[name] = sbuf(name + "_bf16", [P, 512 * PACK], BF16)
-            nc.vector.tensor_copy(
-                rounded[name][:].rearrange("p (t m j) -> p m j t", t=PACK, j=PACK),
-                raw[name][:].rearrange("p j (m t) -> p m j t", t=PACK),
-            )
+        codes = {}
+        scales = {}
 
         def round_weight(name, pair, copy, tag="", first=0, last=P):
             if (name, pair) not in rounded:
                 rounded[name, pair] = sbuf("%s_bf16_%d" % (name, pair), [P, 256 * PACK], BF16, tag)
-            src = raw[name][:].rearrange("p j (m t) -> p m j t", t=PACK)
+            src = raw[name].rearrange("p j (m t) -> p m j t", t=PACK)
             dst = rounded[name, pair][:].rearrange("p (t m j) -> p m j t", t=2, j=PACK)
             copy(dst[:, first:last], src[:, first:last, :, 2 * pair : 2 * pair + 2])
 
         def quantize(out_codes, out_scales, values):
             nc.vector.quantize_mx(out=out_codes.bitcast(FP8X4), scales=out_scales, in_=values)
 
-        def quantize_weight(name, pair):
-            cols = slice(256 * pair, 256 * (pair + 1))
-            quantize(codes[name][:, cols], scales[name][:, cols], rounded[name, pair][:])
-
-        def quantize_whole(name):
-            quantize(codes[name][:], scales[name][:], rounded[name][:])
+        def quantize_weight(name, pair, tag=""):
+            codes[name, pair] = sbuf("%s_codes%d" % (name, pair), [P, 256], U32, tag)
+            scales[name, pair] = sbuf("%s_scales%d" % (name, pair), [P, 256], U8)
+            quantize(codes[name, pair][:], scales[name, pair][:], rounded[name, pair][:])
 
         def multiply(out, name, t, moving_codes, moving_scales, start, stop):
-            cols = slice(t * P, (t + 1) * P)
+            pair, i = divmod(t, 2)
+            cols = slice(i * P, (i + 1) * P)
             nc.tensor.matmul_mx(
                 out=out,
-                lhsT=codes[name][:, cols].bitcast(FP8X4),
-                lhsT_scale=scales[name][:, cols],
+                lhsT=codes[name, pair][:, cols].bitcast(FP8X4),
+                lhsT_scale=scales[name, pair][:, cols],
                 rhs=moving_codes.bitcast(FP8X4),
                 rhs_scale=moving_scales,
                 start=start,
@@ -212,10 +210,17 @@ def tile_picked_zskip_relu_po_kernel(
 
         vector_copy, scalar_copy = nc.vector.tensor_copy, nc.scalar.copy
         gather_scales(0, S)
-        round_weight("w1", 1, scalar_copy)
+        place_scales(0, S)
+        round_weight("w1", 1, scalar_copy, "", 0, 64)
+        round_weight("w1", 1, scalar_copy, "", 64, P)
         round_weight("w1", 0, vector_copy)
+        load_weight("w3", w3, 0, EARLY)
+        load_weight("w2", w2, PACK * 512)
         quantize_weight("w1", 1)
         quantize_weight("w1", 0)
+        warm_bank = bank(7, 2, 256)
+        for i in range(5):
+            multiply(warm_bank[:, i % 2, :], "w1", 0, codes["w1", 0][:], scales["w1", 0][:], True, True)
         gather_words(0, 256)
         gather_words(256, 256)
         gather_words(512, 512)
@@ -230,13 +235,12 @@ def tile_picked_zskip_relu_po_kernel(
             shortcut_product(t, 1, 0, 4 + t)
         round_weight("w2", 0, vector_copy)
         quantize_hidden(0, HALF)
-        codes["w2"] = sbuf("w2_codes", [P, 512], U32, "w1_codes")
         quantize_weight("w2", 0)
         branch_product(0, 1, 0)
         branch_product(1, 1, 0)
-        round_weight("w2", 1, vector_copy, "w1_scales")
+        round_weight("w2", 1, vector_copy)
         quantize_weight("w2", 1)
-        quantize_hidden(512, HALF)
+        quantize_hidden(512, HALF, "raw")
         branch_product(2, 1, 0)
         branch_product(3, 1, 0)
         for c in (0, 256):
@@ -261,8 +265,8 @@ def tile_picked_zskip_relu_po_kernel(
         round_result(512, 256)
         quantize_result(0, HALF)
         store_words(0, HALF)
-        round_result(768, 64)
-        round_result(832, 192, scalar_copy)
+        round_result(768, 32)
+        round_result(800, 224, scalar_copy)
         quantize_result(512, 256)
         quantize_result(768, 256)
         store_words(512, HALF)

@@ -256,7 +256,7 @@ def tile_picked_zskip_relu_po_kernel(
             shortcut_product(t, 1, HALF, t)
             branch_product(t, 1, HALF)
             result_out(t, 1, HALF, scalar_copy)
-            store_result(t, 1, HALF, HALF)
+        store_result(0, 2, HALF, HALF)
         for start, number in ((512, 2), (768, 3)):
             late_product(2, 2, start, number)
             result_out(2, 2, start, scalar_copy)

@@ -153,7 +153,11 @@ def tile_picked_zskip_relu_po_kernel(
             return h_codes[u][:, c : c + count], h_scales[:, start : start + count]
 
         y_banks = {}
-        y_f32 = [sbuf("y_f32%d" % u, [P, PACK, HALF], F32) for u in range(2)]
+        y_space = sbuf("y_f32", [P, PACK * 2560], F32)
+        y_f32 = [
+            y_space[:, 5632:7680].rearrange("p (t s) -> p t s", t=PACK),
+            y_space[:].rearrange("p (t s) -> p t s", t=PACK)[:, :, 0:HALF],
+        ]
         y_bf16 = [sbuf("y_bf16%d" % u, [P, HALF * PACK], BF16) for u in range(2)]
         y_codes = [sbuf("y_codes%d" % u, [P, HALF], I32) for u in range(2)]
         y_scales = sbuf("y_scales", [P, S], U8)
@@ -221,8 +225,8 @@ def tile_picked_zskip_relu_po_kernel(
         warm_bank = bank(7, 2, 256)
         for i in range(5):
             multiply(warm_bank[:, i % 2, :], "w1", 0, codes["w1", 0][:], scales["w1", 0][:], True, True)
-        gather_words(0, 256)
-        gather_words(256, 256)
+        gather_words(0, 128)
+        gather_words(128, 384)
         gather_words(512, 512)
         for b in range(8):
             hidden_product(b, b % 4)
@@ -251,16 +255,15 @@ def tile_picked_zskip_relu_po_kernel(
         result_out(2, 1, 0, scalar_copy)
         store_result(2, 1, 0, HALF)
         result_out(3, 1, 0, vector_copy)
-        store_result(3, 1, 0, HALF)
-        for t in range(2):
-            shortcut_product(t, 1, HALF, t)
+        for number, t in enumerate((3, 0)):
+            shortcut_product(t, 1, HALF, number)
             branch_product(t, 1, HALF)
             result_out(t, 1, HALF, scalar_copy)
-        store_result(0, 2, HALF, HALF)
+        nc.sync.dma_start(out_rows[:, 3, :], y_space[:, 7168:8192])
         for start, number in ((512, 2), (768, 3)):
-            late_product(2, 2, start, number)
-            result_out(2, 2, start, scalar_copy)
-        store_result(2, 2, HALF, HALF)
+            late_product(1, 2, start, number)
+            result_out(1, 2, start, scalar_copy)
+        store_result(0, 3, HALF, HALF)
         round_result(0, HALF)
         round_result(512, 256)
         quantize_result(0, HALF)

@@ -223,8 +223,8 @@ def tile_picked_zskip_relu_po_kernel(
         quantize_weight("w1", 1)
         quantize_weight("w1", 0)
         warm_bank = bank(7, 2, 256)
-        for i in range(5):
-            multiply(warm_bank[:, i % 2, :], "w1", 0, codes["w1", 0][:], scales["w1", 0][:], True, True)
+        for i, count in enumerate((256, 256, 256, 256, 128)):
+            multiply(warm_bank[:, i % 2, 0:count], "w1", 0, codes["w1", 0][:, 0:count], scales["w1", 0][:, 0:count], True, True)
         gather_words(0, 128)
         gather_words(128, 384)
         gather_words(512, 512)
@@ -251,9 +251,8 @@ def tile_picked_zskip_relu_po_kernel(
             scalar_copy(y_f32[0][:, 0, c : c + 256], y_banks[0, 0][:, 0, c : c + 256])
             store_result(0, 1, c, 256)
         result_out(1, 1, 0, vector_copy)
-        store_result(1, 1, 0, HALF)
         result_out(2, 1, 0, scalar_copy)
-        store_result(2, 1, 0, HALF)
+        store_result(1, 2, 0, HALF)
         result_out(3, 1, 0, vector_copy)
         for number, t in enumerate((3, 0)):
             shortcut_product(t, 1, HALF, number)
@@ -275,8 +274,7 @@ def tile_picked_zskip_relu_po_kernel(
         store_words(512, HALF)
 
         for q in range(4):
-            queue = nc.sync if q % 2 == 0 else nc.scalar
-            queue.dma_start(
+            nc.scalar.dma_start(
                 out_2[0, 4 * q : 4 * q + 4, :].bitcast(I32),
                 y_scales[32 * q : 32 * q + 4, :].bitcast(I32),
             )

@@ -153,11 +153,18 @@ def tile_picked_zskip_relu_po_kernel(
             return h_codes[u][:, c : c + count], h_scales[:, start : start + count]
 
         y_banks = {}
-        y_space = sbuf("y_f32", [P, PACK * 2560], F32)
+        y_space = sbuf("y_f32", [P, 8192], F32)
         y_f32 = [
-            y_space[:, 5632:7680].rearrange("p (t s) -> p t s", t=PACK),
-            y_space[:].rearrange("p (t s) -> p t s", t=PACK)[:, :, 0:HALF],
+            y_space[:, 1536:5632].rearrange("p (a e s) -> p a e s", a=2, e=2)[:, :, :, 0:HALF],
+            y_space[:].rearrange("p (a e s) -> p a e s", a=2, e=4)[:, :, 0:2, 0:HALF],
         ]
+        y_first = y_space[:, 1536:5632].rearrange("p (t s) -> p t s", t=PACK)
+
+        def y_rows(first, sums, start, count):
+            u, c = divmod(start, HALF)
+            if u == 0:
+                return y_first[:, first : first + sums, c : c + count]
+            return y_f32[1][:, first // 2, first % 2 : first % 2 + sums, c : c + count]
         y_bf16 = [sbuf("y_bf16%d" % u, [P, HALF * PACK], BF16) for u in range(2)]
         y_codes = [sbuf("y_codes%d" % u, [P, HALF], I32) for u in range(2)]
         y_scales = sbuf("y_scales", [P, S], U8)
@@ -184,20 +191,16 @@ def tile_picked_zskip_relu_po_kernel(
                 multiply(out, "w3", first + i, *x_operand(start, count), False, True)
 
         def result_out(first, sums, start, copy):
-            u, c = divmod(start, HALF)
-            copy(y_f32[u][:, first : first + sums, c : c + HALF // sums], y_banks[first, start][:])
+            copy(y_rows(first, sums, start, HALF // sums), y_banks[first, start][:])
 
         def store_result(first, sums, start, count, queue=nc.sync):
-            u, c = divmod(start, HALF)
-            queue.dma_start(
-                out_rows[:, first : first + sums, start : start + count], y_f32[u][:, first : first + sums, c : c + count]
-            )
+            queue.dma_start(out_rows[:, first : first + sums, start : start + count], y_rows(first, sums, start, count))
 
         def round_result(start, count, copy=nc.vector.tensor_copy):
             u, c = divmod(start, HALF)
             copy(
-                y_bf16[u][:, PACK * c : PACK * (c + count)].rearrange("p (g i t) -> p g t i", i=4, t=PACK),
-                y_f32[u][:, :, c : c + count].rearrange("p t (g i) -> p g t i", i=4),
+                y_bf16[u][:, PACK * c : PACK * (c + count)].rearrange("p (g i a e) -> p g a e i", i=4, a=2, e=2),
+                y_f32[u][:, :, :, c : c + count].rearrange("p a e (g i) -> p g a e i", i=4),
             )
 
         def quantize_result(start, count):
@@ -248,21 +251,21 @@ def tile_picked_zskip_relu_po_kernel(
         branch_product(2, 1, 0)
         branch_product(3, 1, 0)
         for c in (0, 256):
-            scalar_copy(y_f32[0][:, 0, c : c + 256], y_banks[0, 0][:, 0, c : c + 256])
+            scalar_copy(y_first[:, 0, c : c + 256], y_banks[0, 0][:, 0, c : c + 256])
             store_result(0, 1, c, 256)
         result_out(1, 1, 0, vector_copy)
         result_out(2, 1, 0, scalar_copy)
         store_result(1, 2, 0, HALF)
         result_out(3, 1, 0, vector_copy)
-        for number, t in enumerate((3, 0)):
+        for number, t in enumerate((2, 3)):
             shortcut_product(t, 1, HALF, number)
             branch_product(t, 1, HALF)
             result_out(t, 1, HALF, scalar_copy)
-        nc.sync.dma_start(out_rows[:, 3, :], y_space[:, 7168:8192])
+        nc.sync.dma_start(out_0.rearrange("(p t) s -> p (t s)", t=PACK)[:, 2560:4096], y_space[:, 4096:5632])
         for start, number in ((512, 2), (768, 3)):
-            late_product(1, 2, start, number)
-            result_out(1, 2, start, scalar_copy)
-        store_result(0, 3, HALF, HALF)
+            late_product(0, 2, start, number)
+            result_out(0, 2, start, scalar_copy)
+        store_result(0, 2, HALF, HALF)
         round_result(0, HALF)
         round_result(512, 256)
         quantize_result(0, HALF)

@@ -40,7 +40,7 @@ def tile_picked_zskip_relu_po_kernel(
         nc.sync.dma_start(offsets[:], offs)
 
         scale_window = sbuf("scale_window", [P, T], U8)
-        nc.sync.dma_start(scale_window[16:32, :].bitcast(I32), x_scales[0].bitcast(I32))
+        nc.scalar.dma_start(scale_window[16:32, :].bitcast(I32), x_scales[0].bitcast(I32))
         for first, last in ((0, 16), (32, 64), (64, P)):
             nc.vector.memset(scale_window[first:last, :].bitcast(I32), 0)
         x_bytes = sbuf("x_bytes", [P, S], U8)

@@ -19,7 +19,7 @@ PACK = 4
 HALF = 512
 GATHER = 256
 H_TOKENS = 128
-EARLY = 512
+EARLY = 256
 
 
 def tile_picked_zskip_relu_po_kernel(
@@ -218,9 +218,10 @@ def tile_picked_zskip_relu_po_kernel(
         vector_copy, scalar_copy = nc.vector.tensor_copy, nc.scalar.copy
         gather_scales(0, S)
         place_scales(0, S)
-        round_weight("w1", 1, scalar_copy, "", 0, 64)
-        round_weight("w1", 1, scalar_copy, "", 64, P)
-        round_weight("w1", 0, vector_copy)
+        round_weight("w1", 0, scalar_copy, "", 0, 8)
+        round_weight("w1", 1, scalar_copy, "", 0, 8)
+        round_weight("w1", 1, scalar_copy, "", 8, P)
+        round_weight("w1", 0, vector_copy, "", 8, P)
         load_weight("w3", w3, 0, EARLY)
         load_weight("w2", w2, PACK * 512)
         quantize_weight("w1", 1)

from contextlib import ExitStack

import concourse.mybir as mybir

K, T, S, H, N = 512, 2048, 1024, 512, 512
FLOPS = 2 * S * (K * H + H * N + K * N)

F32 = mybir.dt.float32
BF16 = mybir.dt.bfloat16
I32 = mybir.dt.int32
U32 = mybir.dt.uint32
U16 = mybir.dt.uint16
U8 = mybir.dt.uint8
FP8X4 = mybir.dt.float8_e4m3fn_x4
RELU = mybir.ActivationFunctionType.Relu

P = 128
PACK = 4
HALF = 512
GATHER = 256
H_TOKENS = 128
EARLY = 256


def tile_picked_zskip_relu_po_kernel(
    tc, x_words, x_scales, w1, w2, w3, offs, out_0, out_1, out_2
):
    nc = tc.nc
    with ExitStack() as ctx:
        keep = ctx.enter_context(tc.tile_pool(name="keep", bufs=1))
        psum = ctx.enter_context(tc.psum_pool(name="psum", bufs=1))

        def sbuf(name, shape, dtype, tag=""):
            return keep.tile(shape, dtype, name=name, tag=tag or name, align_bytes=64)

        def bank(number, sums, tokens):
            return psum.tile([P, sums, tokens], F32, name="bank", tag="bank%d" % number)

        offsets = keep.tile([P, S // 16], U16, name="offsets")
        nc.sync.dma_start(offsets[:], offs)

        scale_window = sbuf("scale_window", [P, T], U8)
        nc.scalar.dma_start(scale_window[16:32, :].bitcast(I32), x_scales[0].bitcast(I32))
        for first, last in ((0, 16), (32, 64), (64, P)):
            nc.vector.memset(scale_window[first:last, :].bitcast(I32), 0)
        x_bytes = sbuf("x_bytes", [P, S], U8)
        nc.vector.memset(x_bytes[:].bitcast(I32), 0)

        space = sbuf("raw", [P, 2 * PACK * 512], F32)
        raw = {}

        def load_weight(name, w, offset, first=0, last=PACK * 512):
            raw[name] = space[:, offset : offset + PACK * 512].rearrange("p (j c) -> p j c", j=PACK)
            rows = w.rearrange("(p j) c -> p (j c)", j=PACK)
            nc.sync.dma_start(space[:, offset + first : offset + last], rows[:, first:last])

        word_window = sbuf("word_window", [P, T], I32)
        load_weight("w1", w1, PACK * 512 - 32)
        nc.sync.dma_start(word_window[:], x_words[0].rearrange("p n t -> p (n t)").bitcast(I32))
        load_weight("w3", w3, 0, 0, EARLY)

        warm = sbuf("warm", [P, 1], F32)
        nc.gpsimd.memset(warm[:], 0.0)
        warm_out = sbuf("warm_out", [P, 1], F32)
        nc.scalar.activation(warm_out[:], warm[:], RELU)

        x_codes = [sbuf("x_codes%d" % u, [P, HALF], U32) for u in range(2)]
        picked_bytes = sbuf("picked_bytes", [P, S], U8)

        def place_scales(start, count):
            for q in range(4):
                nc.sync.dma_start(
                    x_bytes[32 * q : 32 * q + 4, start : start + count].bitcast(I32),
                    picked_bytes[16 + 4 * q : 20 + 4 * q, start : start + count].bitcast(I32),
                )

        def gather_scales(start, count):
            nc.vector.tensor_copy(
                picked_bytes[:, start : start + count],
                scale_window[:].indirect(offsets[:, start // 16 : (start + count) // 16]),
            )

        def gather_words(start, count):
            u, c = divmod(start, HALF)
            nc.vector.tensor_copy(
                x_codes[u][:, c : c + count],
                word_window[:].bitcast(U32).indirect(offsets[:, start // 16 : (start + count) // 16]),
            )

        rounded = {}
        codes = {}
        scales = {}

        def round_weight(name, pair, copy, tag="", first=0, last=P):
            if (name, pair) not in rounded:
                rounded[name, pair] = sbuf("%s_bf16_%d" % (name, pair), [P, 256 * PACK], BF16, tag)
            src = raw[name].rearrange("p j (m t) -> p m j t", t=PACK)
            dst = rounded[name, pair][:].rearrange("p (t m j) -> p m j t", t=2, j=PACK)
            copy(dst[:, first:last], src[:, first:last, :, 2 * pair : 2 * pair + 2])

        def quantize(out_codes, out_scales, values):
            nc.vector.quantize_mx(out=out_codes.bitcast(FP8X4), scales=out_scales, in_=values)

        def quantize_weight(name, pair, tag=""):
            codes[name, pair] = sbuf("%s_codes%d" % (name, pair), [P, 256], U32, tag)
            scales[name, pair] = sbuf("%s_scales%d" % (name, pair), [P, 256], U8)
            quantize(codes[name, pair][:], scales[name, pair][:], rounded[name, pair][:])

        def multiply(out, name, t, moving_codes, moving_scales, start, stop):
            pair, i = divmod(t, 2)
            cols = slice(i * P, (i + 1) * P)
            nc.tensor.matmul_mx(
                out=out,
                lhsT=codes[name, pair][:, cols].bitcast(FP8X4),
                lhsT_scale=scales[name, pair][:, cols],
                rhs=moving_codes.bitcast(FP8X4),
                rhs_scale=moving_scales,
                start=start,
                stop=stop,
            )

        def x_operand(start, count):
            u, c = divmod(start, HALF)
            return x_codes[u][:, c : c + count], x_bytes[:, start : start + count]

        h_bf16 = [sbuf("h_bf16%d" % u, [P, HALF * PACK], BF16) for u in range(2)]
        h_codes = {}
        h_scales = sbuf("h_scales", [P, S], U8)
        h_banks = {}

        def hidden_product(b, number):
            h_banks[b] = bank(number, PACK, H_TOKENS)
            for t in range(PACK):
                multiply(h_banks[b][:, t, :], "w1", t, *x_operand(b * H_TOKENS, H_TOKENS), True, True)

        def hidden_out(b, on_vector=False):
            u, c = divmod(b * H_TOKENS, HALF)
            dst = h_bf16[u][:, PACK * c : PACK * (c + H_TOKENS)].rearrange("p (n t) -> p n t", t=PACK)
            src = h_banks[b][:].rearrange("p t n -> p n t")
            if on_vector:
                nc.vector.tensor_scalar_max(dst, src, 0.0)
            else:
                nc.scalar.activation(dst, src, RELU)

        def quantize_hidden(start, count, tag=""):
            u, c = divmod(start, HALF)
            if u not in h_codes:
                h_codes[u] = sbuf("h_codes%d" % u, [P, HALF], U32, tag)
            quantize(h_codes[u][:, c : c + count], h_scales[:, start : start + count], h_bf16[u][:, PACK * c : PACK * (c + count)])

        def h_operand(start, count):
            u, c = divmod(start, HALF)
            return h_codes[u][:, c : c + count], h_scales[:, start : start + count]

        y_banks = {}
        y_space = sbuf("y_f32", [P, 8192], F32)
        y_f32 = [
            y_space[:, 1536:5632].rearrange("p (a e s) -> p a e s", a=2, e=2)[:, :, :, 0:HALF],
            y_space[:].rearrange("p (a e s) -> p a e s", a=2, e=4)[:, :, 0:2, 0:HALF],
        ]
        y_first = y_space[:, 1536:5632].rearrange("p (t s) -> p t s", t=PACK)

        def y_rows(first, sums, start, count):
            u, c = divmod(start, HALF)
            if u == 0:
                return y_first[:, first : first + sums, c : c + count]
            return y_f32[1][:, first // 2, first % 2 : first % 2 + sums, c : c + count]
        y_bf16 = [sbuf("y_bf16%d" % u, [P, HALF * PACK], BF16) for u in range(2)]
        y_codes = [sbuf("y_codes%d" % u, [P, HALF], I32) for u in range(2)]
        y_scales = sbuf("y_scales", [P, S], U8)
        out_rows = out_0.rearrange("(p t) s -> p t s", t=PACK)
        out_words = out_1[0].rearrange("p n t -> p (n t)").bitcast(I32)

        def shortcut_product(first, sums, start, number):
            count = HALF // sums
            y_banks[first, start] = bank(number, sums, count)
            for i in range(sums):
                multiply(y_banks[first, start][:, i, :], "w3", first + i, *x_operand(start, count), i == 0, False)

        def branch_product(first, sums, start):
            count = HALF // sums
            for i in range(sums):
                multiply(y_banks[first, start][:, i, :], "w2", first + i, *h_operand(start, count), False, i == sums - 1)

        def late_product(first, sums, start, number):
            count = HALF // sums
            y_banks[first, start] = bank(number, sums, count)
            for i in range(sums):
                out = y_banks[first, start][:, i, :]
                multiply(out, "w2", first + i, *h_operand(start, count), True, False)
                multiply(out, "w3", first + i, *x_operand(start, count), False, True)

        def result_out(first, sums, start, copy):
            copy(y_rows(first, sums, start, HALF // sums), y_banks[first, start][:])

        def store_result(first, sums, start, count, queue=nc.sync):
            queue.dma_start(out_rows[:, first : first + sums, start : start + count], y_rows(first, sums, start, count))

        def round_result(start, count, copy=nc.vector.tensor_copy):
            u, c = divmod(start, HALF)
            copy(
                y_bf16[u][:, PACK * c : PACK * (c + count)].rearrange("p (g i a e) -> p g a e i", i=4, a=2, e=2),
                y_f32[u][:, :, :, c : c + count].rearrange("p a e (g i) -> p g a e i", i=4),
            )

        def quantize_result(start, count):
            u, c = divmod(start, HALF)
            quantize(
                y_codes[u][:, c : c + count],
                y_scales[:, start : start + count],
                y_bf16[u][:, PACK * c : PACK * (c + count)],
            )

        def store_words(start, count, queue=nc.sync):
            u, c = divmod(start, HALF)
            queue.dma_start(out_words[:, start : start + count], y_codes[u][:, c : c + count])

        vector_copy, scalar_copy = nc.vector.tensor_copy, nc.scalar.copy
        gather_scales(0, S)
        place_scales(0, S)
        round_weight("w1", 0, scalar_copy, "", 0, 8)
        round_weight("w1", 1, scalar_copy, "", 0, 8)
        round_weight("w1", 1, scalar_copy, "", 8, P)
        round_weight("w1", 0, vector_copy, "", 8, P)
        load_weight("w3", w3, 0, EARLY)
        load_weight("w2", w2, PACK * 512)
        quantize_weight("w1", 1)
        quantize_weight("w1", 0)
        warm_bank = bank(7, 2, 256)
        for i, count in enumerate((256, 256, 256, 256, 128)):
            multiply(warm_bank[:, i % 2, 0:count], "w1", 0, codes["w1", 0][:, 0:count], scales["w1", 0][:, 0:count], True, True)
        gather_words(0, 128)
        gather_words(128, 384)
        gather_words(512, 512)
        for b in range(8):
            hidden_product(b, b % 4)
            hidden_out(b)
        round_weight("w3", 0, vector_copy)
        round_weight("w3", 1, vector_copy)
        quantize_weight("w3", 0)
        quantize_weight("w3", 1)
        for t in range(PACK):
            shortcut_product(t, 1, 0, 4 + t)
        round_weight("w2", 0, vector_copy)
        quantize_hidden(0, HALF)
        quantize_weight("w2", 0)
        branch_product(0, 1, 0)
        branch_product(1, 1, 0)
        round_weight("w2", 1, vector_copy)
        quantize_weight("w2", 1)
        quantize_hidden(512, HALF, "raw")
        branch_product(2, 1, 0)
        branch_product(3, 1, 0)
        for c in (0, 256):
            scalar_copy(y_first[:, 0, c : c + 256], y_banks[0, 0][:, 0, c : c + 256])
            store_result(0, 1, c, 256)
        result_out(1, 1, 0, vector_copy)
        result_out(2, 1, 0, scalar_copy)
        store_result(1, 2, 0, HALF)
        result_out(3, 1, 0, vector_copy)
        for number, t in enumerate((2, 3)):
            shortcut_product(t, 1, HALF, number)
            branch_product(t, 1, HALF)
            result_out(t, 1, HALF, scalar_copy)
        nc.sync.dma_start(out_0.rearrange("(p t) s -> p (t s)", t=PACK)[:, 2560:4096], y_space[:, 4096:5632])
        for start, number in ((512, 2), (768, 3)):
            late_product(0, 2, start, number)
            result_out(0, 2, start, scalar_copy)
        store_result(0, 2, HALF, HALF)
        round_result(0, HALF)
        round_result(512, 256)
        quantize_result(0, HALF)
        store_words(0, HALF)
        round_result(768, 32)
        round_result(800, 224, scalar_copy)
        quantize_result(512, 256)
        quantize_result(768, 256)
        store_words(512, HALF)

        for q in range(4):
            nc.scalar.dma_start(
                out_2[0, 4 * q : 4 * q + 4, :].bitcast(I32),
                y_scales[32 * q : 32 * q + 4, :].bitcast(I32),
            )
